import numpy as np
import ml_dtypes

BF16 = ml_dtypes.bfloat16


def bf(x):
    return np.asarray(x, np.float32).astype(BF16)


def f32(x):
    return np.asarray(x, np.float32)


def f64(x):
    return np.asarray(x).astype(np.float64)


def striped(idx):
    return np.tile(idx.reshape(-1, 16).T, (8, 1))


def rows(idx, k):
    return np.tile(idx, (k, 1))


def look(tab, idx):
    return np.take_along_axis(f64(tab), rows(idx, len(tab)), axis=1)


K, S, V, N, M = 512, 256, 256, 256, 128


def setup_inputs():
    return {"tab": f32(np.random.standard_normal((K, S))), "w": bf(np.random.standard_normal((K, M)) / np.sqrt(K)), "b": f32(0.5 * np.random.standard_normal((M, 1))), "offs": striped(np.random.randint(0, S, N))}


def reference(tab, w, b, offs):
    idx = offs[:16].T.reshape(-1)
    t = look(tab, idx)
    x = (t >= 0.25) * 0.5
    y = f64(w).T @ x
    return np.maximum(y + f64(b), 0.0)

@@ -1,0 +1,65 @@
+import concourse.mybir as mybir
+
+F32, BF16, U16 = mybir.dt.float32, mybir.dt.bfloat16, mybir.dt.uint16
+IS_GE, MULT = mybir.AluOpType.is_ge, mybir.AluOpType.mult
+RELU = mybir.ActivationFunctionType.Relu
+
+P = 128
+K, S, N, M = 512, 256, 256, 128
+BLOCKS = K // P
+PIECE = 128
+PIECES = N // PIECE
+COLUMNS = PIECE // 16
+
+FLOPS = 2 * K * M * N
+
+
+def tile_lookup_deq_step_relu_kernel(tc, tab, w, b, offs, out):
+    nc = tc.nc
+    tab_blocks = tab.rearrange("(p block) s -> block p s", block=BLOCKS)
+    w_rows = w.rearrange("(p block) m -> p (block m)", block=BLOCKS)
+
+    with (
+        tc.tile_pool(name="held", bufs=1) as held,
+        tc.psum_pool(name="psum", bufs=1) as psum,
+    ):
+        offsets = held.tile([P, N // 16], U16, name="offsets")
+        nc.sync.dma_start(offsets[:], offs)
+        windows = []
+        for block in range(BLOCKS):
+            window = held.tile([P, S], F32, name=f"window{block}")
+            nc.sync.dma_start(window[:], tab_blocks[block])
+            windows.append(window)
+
+        weights = held.tile([P, BLOCKS * M], BF16, name="weights")
+        nc.scalar.dma_start(weights[:], w_rows)
+        bias = held.tile([P, 1], F32, name="bias")
+        nc.scalar.dma_start(bias[:], b)
+
+        sums = [psum.tile([M, PIECE], F32, name=f"sums{piece}") for piece in range(PIECES)]
+
+        for block in range(BLOCKS):
+            for piece in range(PIECES):
+                step = held.tile([P, PIECE], F32, name=f"step{block}_{piece}")
+                nc.vector.tensor_scalar(
+                    step[:],
+                    windows[block][:].indirect(offsets[:, piece * COLUMNS : (piece + 1) * COLUMNS]),
+                    scalar1=0.25,
+                    scalar2=0.5,
+                    op0=IS_GE,
+                    op1=MULT,
+                )
+                step_bf16 = held.tile([P, PIECE], BF16, name=f"step_bf16_{block}_{piece}")
+                nc.scalar.copy(step_bf16[:], step[:])
+                nc.tensor.matmul(
+                    sums[piece][:],
+                    weights[:, block * M : (block + 1) * M],
+                    step_bf16[:],
+                    start=(block == 0),
+                    stop=(block == BLOCKS - 1),
+                )
+
+        for piece in range(PIECES):
+            result = held.tile([M, PIECE], F32, name=f"result{piece}")
+            nc.scalar.activation(result[:], sums[piece][:], RELU, bias=bias[:])
+            nc.sync.dma_start(out[:, piece * PIECE : (piece + 1) * PIECE], result[:])

@@ -49,12 +49,11 @@ def tile_lookup_deq_step_relu_kernel(tc, tab, w, b, offs, out):
                     op0=IS_GE,
                     op1=MULT,
                 )
-                step_bf16 = held.tile([P, PIECE], BF16, name=f"step_bf16_{block}_{piece}")
-                nc.scalar.copy(step_bf16[:], step[:])
+                step_bf16 = step[:].bitcast(BF16)[:, 1::2]
                 nc.tensor.matmul(
                     sums[piece][:],
                     weights[:, block * M : (block + 1) * M],
-                    step_bf16[:],
+                    step_bf16,
                     start=(block == 0),
                     stop=(block == BLOCKS - 1),
                 )

@@ -27,8 +27,9 @@ def tile_lookup_deq_step_relu_kernel(tc, tab, w, b, offs, out):
         nc.sync.dma_start(offsets[:], offs)
         windows = []
         for block in range(BLOCKS):
+            queue = nc.scalar if block % 2 == 0 else nc.sync
             window = held.tile([P, S], F32, name=f"window{block}")
-            nc.sync.dma_start(window[:], tab_blocks[block])
+            queue.dma_start(window[:], tab_blocks[block])
             windows.append(window)
 
         weights = held.tile([P, BLOCKS * M], BF16, name="weights")

@@ -2,6 +2,7 @@ import concourse.mybir as mybir
 
 F32, BF16, U16 = mybir.dt.float32, mybir.dt.bfloat16, mybir.dt.uint16
 IS_GE, MULT = mybir.AluOpType.is_ge, mybir.AluOpType.mult
+ADD, MAX = mybir.AluOpType.add, mybir.AluOpType.max
 RELU = mybir.ActivationFunctionType.Relu
 
 P = 128
@@ -61,5 +62,9 @@ def tile_lookup_deq_step_relu_kernel(tc, tab, w, b, offs, out):
 
         for piece in range(PIECES):
             result = held.tile([M, PIECE], F32, name=f"result{piece}")
-            nc.scalar.activation(result[:], sums[piece][:], RELU, bias=bias[:])
-            nc.sync.dma_start(out[:, piece * PIECE : (piece + 1) * PIECE], result[:])
+            if piece < PIECES - 1:
+                nc.scalar.activation(result[:], sums[piece][:], RELU, bias=bias[:])
+                nc.scalar.dma_start(out[:, piece * PIECE : (piece + 1) * PIECE], result[:])
+            else:
+                nc.vector.tensor_scalar(result[:], sums[piece][:], scalar1=bias[:], scalar2=0.0, op0=ADD, op1=MAX)
+                nc.sync.dma_start(out[:, piece * PIECE : (piece + 1) * PIECE], result[:])

import concourse.mybir as mybir

F32, BF16, U16 = mybir.dt.float32, mybir.dt.bfloat16, mybir.dt.uint16
IS_GE, MULT = mybir.AluOpType.is_ge, mybir.AluOpType.mult
ADD, MAX = mybir.AluOpType.add, mybir.AluOpType.max
RELU = mybir.ActivationFunctionType.Relu

P = 128
K, S, N, M = 512, 256, 256, 128
BLOCKS = K // P
PIECE = 128
PIECES = N // PIECE
COLUMNS = PIECE // 16

FLOPS = 2 * K * M * N


def tile_lookup_deq_step_relu_kernel(tc, tab, w, b, offs, out):
    nc = tc.nc
    tab_blocks = tab.rearrange("(p block) s -> block p s", block=BLOCKS)
    w_rows = w.rearrange("(p block) m -> p (block m)", block=BLOCKS)

    with (
        tc.tile_pool(name="held", bufs=1) as held,
        tc.psum_pool(name="psum", bufs=1) as psum,
    ):
        offsets = held.tile([P, N // 16], U16, name="offsets")
        nc.sync.dma_start(offsets[:], offs)
        windows = []
        for block in range(BLOCKS):
            queue = nc.scalar if block % 2 == 0 else nc.sync
            window = held.tile([P, S], F32, name=f"window{block}")
            queue.dma_start(window[:], tab_blocks[block])
            windows.append(window)

        weights = held.tile([P, BLOCKS * M], BF16, name="weights")
        nc.scalar.dma_start(weights[:], w_rows)
        bias = held.tile([P, 1], F32, name="bias")
        nc.scalar.dma_start(bias[:], b)

        sums = [psum.tile([M, PIECE], F32, name=f"sums{piece}") for piece in range(PIECES)]

        for block in range(BLOCKS):
            for piece in range(PIECES):
                step = held.tile([P, PIECE], F32, name=f"step{block}_{piece}")
                nc.vector.tensor_scalar(
                    step[:],
                    windows[block][:].indirect(offsets[:, piece * COLUMNS : (piece + 1) * COLUMNS]),
                    scalar1=0.25,
                    scalar2=0.5,
                    op0=IS_GE,
                    op1=MULT,
                )
                step_bf16 = step[:].bitcast(BF16)[:, 1::2]
                nc.tensor.matmul(
                    sums[piece][:],
                    weights[:, block * M : (block + 1) * M],
                    step_bf16,
                    start=(block == 0),
                    stop=(block == BLOCKS - 1),
                )

        for piece in range(PIECES):
            result = held.tile([M, PIECE], F32, name=f"result{piece}")
            if piece < PIECES - 1:
                nc.scalar.activation(result[:], sums[piece][:], RELU, bias=bias[:])
                nc.scalar.dma_start(out[:, piece * PIECE : (piece + 1) * PIECE], result[:])
            else:
                nc.vector.tensor_scalar(result[:], sums[piece][:], scalar1=bias[:], scalar2=0.0, op0=ADD, op1=MAX)
                nc.sync.dma_start(out[:, piece * PIECE : (piece + 1) * PIECE], result[:])
